import numpy as np
import ml_dtypes


def mxq(x, axis, fmt="e4m3"):
    dtype, down = {"e4m3": (ml_dtypes.float8_e4m3fn, 7), "e5m2": (ml_dtypes.float8_e5m2, 14)}[fmt]
    v = np.moveaxis(np.asarray(x, np.float32).astype(ml_dtypes.bfloat16).astype(np.float64), axis, -1)
    blocks = v.reshape(v.shape[:-1] + (-1, 32))
    amax = np.abs(blocks).max(-1, keepdims=True)
    byte = np.maximum(np.where(amax > 0, np.frexp(amax)[1] - 1 + 127, 0) - down, 1)
    scale = np.exp2(byte - 127.0)
    codes = (blocks / scale).astype(np.float32).astype(dtype).astype(np.float64)
    return np.moveaxis((codes * scale).reshape(v.shape), -1, axis)


WIDE = False


def mx_kscale(k, group=512):
    if not WIDE:
        return np.ones(k)
    levels = np.array([18, -18])
    if group != 512:
        return np.exp2(np.random.permutation(np.resize(levels, k // group))).repeat(group)
    if k % 512:
        return np.exp2(np.random.permutation(np.resize(levels, k // 32))).repeat(32)
    a = np.empty((k // 512, 16))
    for p in range(k // 512):
        a[p, :8] = np.random.permutation(np.resize(levels, 8))
        for g in range(8):
            far = levels[np.abs(levels - a[p, g]) >= 10]
            a[p, g + 8] = far[np.random.randint(len(far))]
    return np.exp2(a.ravel()).repeat(32)


def f64(x):
    return np.asarray(x).astype(np.float64)


G, D, M, O, N = 4, 128, 128, 128, 512


def sgn(shape):
    return np.random.uniform(0.5, 2.0, shape) * np.where(np.random.standard_normal(shape) < 0, -1.0, 1.0)


def setup_inputs():
    n = np.random.standard_normal
    s_d = mx_kscale(D, 0)
    s_m = mx_kscale(M, 0)
    return {
        "x": (n((G, D, N)) * s_d[:, None]).astype(np.float32),
        "w1": (n((G, D, M)) / np.sqrt(D) / s_d[:, None]).astype(np.float32),
        "w2": (n((G, D, M)) / np.sqrt(D) / s_d[:, None]).astype(np.float32),
        "so": (np.random.uniform(0.3, 1.0, (G, M, 1))).astype(np.float32),
        "hs": (sgn((G, M, 1)) * s_m[:, None]).astype(np.float32),
        "wo2": (n((G, M, O)) / np.sqrt(M) / s_m[:, None]).astype(np.float32),
        "res": (0.5 * n((G, O, N))).astype(np.float32),
    }


def reference(x, w1, w2, so, hs, wo2, res):
    w1q = mxq(f64(w1), 1, "e4m3")
    xq = mxq(f64(x), 1, "e4m3")
    z1 = w1q.transpose(0, 2, 1) @ xq
    w2q = mxq(f64(w2), 1, "e4m3")
    z2 = w2q.transpose(0, 2, 1) @ xq
    nm = np.sqrt(np.square(z1) * np.square(z2) + f64(so))
    h = z1 * z2 / nm
    hh = h * f64(hs)
    wo2q = mxq(f64(wo2), 1, "e4m3")
    hhq = mxq(hh, 1, "e4m3")
    y0 = wo2q.transpose(0, 2, 1) @ hhq
    y = y0 + f64(res)
    return y

@@ -1,0 +1,177 @@
+from contextlib import ExitStack
+
+import concourse.mybir as mybir
+
+G, D, M, O, N = 4, 128, 128, 128, 512
+FLOPS = 2 * G * N * (2 * D * M + M * O)
+
+F32 = mybir.dt.float32
+BF16 = mybir.dt.bfloat16
+U32 = mybir.dt.uint32
+U8 = mybir.dt.uint8
+FP8X4 = mybir.dt.float8_e4m3fn_x4
+ACT = mybir.ActivationFunctionType
+ALU = mybir.AluOpType
+
+P = 128
+PACK = 4
+ROWS = 32
+PASS = 128
+CHUNKS = (128, 128, 128, 128)
+SQUARES_ON_SCALAR = (4, 4, 4, 3)
+
+
+def tile_rows_fagree_kernel(tc, x, w1, w2, so, hs, wo2, res, out):
+    nc = tc.nc
+    starts = [sum(CHUNKS[:c]) for c in range(len(CHUNKS))]
+    last = len(CHUNKS) - 1
+
+    with ExitStack() as ctx:
+        sb = ctx.enter_context(tc.tile_pool(name="sb", bufs=1))
+        ps = ctx.enter_context(tc.psum_pool(name="ps", bufs=1))
+        ctx.enter_context(tc.manual_schedule())
+
+        def rows_of(g):
+            return slice(ROWS * g, ROWS * (g + 1))
+
+        def load_packed(name, src, width):
+            raw = sb.tile([P, PACK, width], F32, name=name + "_raw", align_bytes=64)
+            nc.sync.dma_start(out=raw[:], in_=src)
+            return raw
+
+        def interleave(copy, name, raw, width):
+            grouped = sb.tile([P, width, PACK], BF16, name=name + "_grouped", align_bytes=64)
+            copy(
+                out=grouped[:].rearrange("p (c i) j -> p c j i", i=4),
+                in_=raw[:].rearrange("p j (c i) -> p c j i", i=4),
+            )
+            return grouped
+
+        def quantise(name, grouped, width):
+            codes = sb.tile([P, width], U32, name=name + "_codes", align_bytes=64)
+            scales = sb.tile([P, width], U8, name=name + "_scales", align_bytes=64)
+            nc.vector.quantize_mx(
+                out=codes[:].bitcast(FP8X4),
+                scales=scales[:],
+                in_=grouped[:].rearrange("p w j -> p (w j)"),
+            )
+            return codes, scales
+
+        def product(banks, weights, moving, width):
+            for n0 in range(0, width, PASS):
+                cols = slice(n0, n0 + PASS)
+                for g in range(G):
+                    r = rows_of(g)
+                    nc.tensor.matmul_mx(
+                        out=banks[g][:, cols],
+                        lhsT=weights[0][r, :].bitcast(FP8X4),
+                        lhsT_scale=weights[1][r, :],
+                        rhs=moving[0][r, cols].bitcast(FP8X4),
+                        rhs_scale=moving[1][r, cols],
+                        start=True,
+                        stop=True,
+                    )
+
+        bank_a = [ps.tile([P, 512], F32, name="bank_a%d" % g) for g in range(G)]
+        bank_b = [ps.tile([P, 512], F32, name="bank_b%d" % g) for g in range(G)]
+
+        const_rows = sb.tile([P, 2 * M], F32, name="const_rows", align_bytes=64)
+        nc.vector.memset(const_rows[:], 0.0)
+        warm_in = sb.tile([P, 1], F32, name="warm_in")
+        warm_out = sb.tile([P, 1], F32, name="warm_out")
+        nc.gpsimd.memset(warm_in[:], 1.0)
+        nc.scalar.activation(out=warm_out[:], in_=warm_in[:], func=ACT.Abs_reciprocal_sqrt)
+
+        x_packed = x.rearrange("g (p j) n -> (g p) j n", j=PACK)
+        w1_raw = load_packed("w1", w1.rearrange("g (p j) m -> (g p) j m", j=PACK), M)
+        x_raw = [load_packed("x0", x_packed[:, :, 0 : CHUNKS[0]], CHUNKS[0])]
+        w2_raw = load_packed("w2", w2.rearrange("g (p j) m -> (g p) j m", j=PACK), M)
+        for k, vec in enumerate((so, hs)):
+            nc.sync.dma_start(
+                out=const_rows[0:P:ROWS, k * M : (k + 1) * M].rearrange("a (g i) -> a g i", g=G),
+                in_=vec.rearrange("g (a i) o -> a g (i o)", i=ROWS),
+            )
+        for c in range(1, last + 1):
+            x_raw.append(load_packed("x%d" % c, x_packed[:, :, starts[c] : starts[c] + CHUNKS[c]], CHUNKS[c]))
+        wo_raw = load_packed("wo", wo2.rearrange("g (p j) o -> (g p) j o", j=PACK), O)
+        res_sb = sb.tile([P, G, N], F32, name="res_sb")
+        nc.sync.dma_start(out=res_sb[:], in_=res.rearrange("g o n -> o g n"))
+
+        w1_grouped = interleave(nc.vector.tensor_copy, "w1", w1_raw, M)
+        x_grouped = interleave(nc.scalar.copy, "x0", x_raw[0], CHUNKS[0])
+        w1_q = quantise("w1", w1_grouped, M)
+        x_q = quantise("x0", x_grouped, CHUNKS[0])
+        w2_grouped = interleave(nc.vector.tensor_copy, "w2", w2_raw, M)
+        product(bank_a, w1_q, x_q, CHUNKS[0])
+        consts = sb.tile([P, 2 * M], F32, name="consts", align_bytes=64)
+        w2_q = quantise("w2", w2_grouped, M)
+        product(bank_b, w2_q, x_q, CHUNKS[0])
+        nc.vector.transpose(out=consts[:], in_=const_rows[:])
+
+        planes = []
+        wo_q = None
+        for c, width in enumerate(CHUNKS):
+            z1, prod, sq, inv = [], [], [], []
+            for g in range(G):
+                t = sb.tile([P, width], F32, name="z1_%d_%d" % (c, g))
+                nc.scalar.copy(out=t[:], in_=bank_a[g][:, 0:width])
+                z1.append(t)
+            for g in range(G):
+                t = sb.tile([P, width], F32, name="prod_%d_%d" % (c, g))
+                nc.vector.tensor_tensor(out=t[:], in0=bank_b[g][:, 0:width], in1=z1[g][:], op=ALU.mult)
+                prod.append(t)
+            if c < last:
+                ahead = interleave(nc.vector.tensor_copy, "x%d" % (c + 1), x_raw[c + 1], CHUNKS[c + 1])
+            else:
+                ahead = interleave(nc.vector.tensor_copy, "wo", wo_raw, O)
+            for g in range(G):
+                t = sb.tile([P, width], F32, name="sq_%d_%d" % (c, g))
+                if g < SQUARES_ON_SCALAR[c]:
+                    nc.scalar.activation(out=t[:], in_=prod[g][:], func=ACT.Square)
+                else:
+                    nc.vector.tensor_tensor(out=t[:], in0=prod[g][:], in1=prod[g][:], op=ALU.mult)
+                sq.append(t)
+            if c < last:
+                x_q = quantise("x%d" % (c + 1), ahead, CHUNKS[c + 1])
+                product(bank_a, w1_q, x_q, CHUNKS[c + 1])
+                product(bank_b, w2_q, x_q, CHUNKS[c + 1])
+            else:
+                wo_q = quantise("wo", ahead, O)
+            for g in range(G):
+                t = sb.tile([P, width], F32, name="inv_%d_%d" % (c, g))
+                nc.scalar.activation(
+                    out=t[:], in_=sq[g][:], func=ACT.Abs_reciprocal_sqrt,
+                    bias=consts[:, ROWS * g : ROWS * g + 1],
+                )
+                inv.append(t)
+            plane = sb.tile([P, PACK, width], BF16, name="planes_%d" % c, align_bytes=64)
+            for g in range(G):
+                t = sb.tile([P, width], BF16, name="hh_%d_%d" % (c, g), align_bytes=64)
+                nc.vector.scalar_tensor_tensor(
+                    out=t[:], in0=prod[g][:], scalar=consts[:, M + ROWS * g : M + ROWS * g + 1],
+                    in1=inv[g][:], op0=ALU.mult, op1=ALU.mult,
+                )
+                nc.sync.dma_start(out=plane[rows_of(g), :, :], in_=t[:])
+            planes.append(plane)
+
+        out_view = out.rearrange("g o n -> o g n")
+
+        def second(c, grouped):
+            hh_q = quantise("hh%d" % c, grouped, CHUNKS[c])
+            product(bank_a if c % 2 == 0 else bank_b, wo_q, hh_q, CHUNKS[c])
+
+        def finish(c):
+            width = CHUNKS[c]
+            banks = bank_a if c % 2 == 0 else bank_b
+            cols = slice(starts[c], starts[c] + width)
+            y = sb.tile([P, G, width], F32, name="y_%d" % c)
+            for g in range(G):
+                nc.vector.tensor_tensor(out=y[:, g, :], in0=banks[g][:, 0:width], in1=res_sb[:, g, cols], op=ALU.add)
+            nc.sync.dma_start(out=out_view[:, :, cols], in_=y[:])
+
+        grouped = [interleave(nc.scalar.copy, "hh%d" % c, planes[c], CHUNKS[c]) for c in range(last + 1)]
+        second(0, grouped[0])
+        for c in range(1, last + 1):
+            second(c, grouped[c])
+            finish(c - 1)
+        finish(last)

@@ -16,15 +16,19 @@ ALU = mybir.AluOpType
 P = 128
 PACK = 4
 ROWS = 32
-PASS = 128
-CHUNKS = (128, 128, 128, 128)
-SQUARES_ON_SCALAR = (4, 4, 4, 3)
+W = 128
+CHUNKS = N // W
+BANK = 512
+RUN = 4
+VECTOR_SHARE = 80
+HALF = G // 2
+ALL_GROUPS = range(G)
+FIRST_GROUPS = range(HALF)
+LAST_GROUPS = range(HALF, G)
 
 
 def tile_rows_fagree_kernel(tc, x, w1, w2, so, hs, wo2, res, out):
     nc = tc.nc
-    starts = [sum(CHUNKS[:c]) for c in range(len(CHUNKS))]
-    last = len(CHUNKS) - 1
 
     with ExitStack() as ctx:
         sb = ctx.enter_context(tc.tile_pool(name="sb", bufs=1))
@@ -34,144 +38,205 @@ def tile_rows_fagree_kernel(tc, x, w1, w2, so, hs, wo2, res, out):
         def rows_of(g):
             return slice(ROWS * g, ROWS * (g + 1))
 
-        def load_packed(name, src, width):
-            raw = sb.tile([P, PACK, width], F32, name=name + "_raw", align_bytes=64)
-            nc.sync.dma_start(out=raw[:], in_=src)
-            return raw
+        def load_rows(name, src, width):
+            rows = sb.tile([P, PACK, width], F32, name=name + "_rows", align_bytes=64)
+            nc.sync.dma_start(out=rows[:], in_=src)
+            return rows
 
-        def interleave(copy, name, raw, width):
-            grouped = sb.tile([P, width, PACK], BF16, name=name + "_grouped", align_bytes=64)
+        def word_tile(name):
+            return sb.tile([P, W, PACK], BF16, name=name + "_words", align_bytes=64)
+
+        def interleave(copy, words, rows, lo, hi):
             copy(
-                out=grouped[:].rearrange("p (c i) j -> p c j i", i=4),
-                in_=raw[:].rearrange("p j (c i) -> p c j i", i=4),
+                out=words[:, lo:hi, :].rearrange("p (c i) j -> p c j i", i=RUN),
+                in_=rows[:, :, lo:hi].rearrange("p j (c i) -> p c j i", i=RUN),
             )
-            return grouped
 
-        def quantise(name, grouped, width):
-            codes = sb.tile([P, width], U32, name=name + "_codes", align_bytes=64)
-            scales = sb.tile([P, width], U8, name=name + "_scales", align_bytes=64)
+        def interleave_shared(words, rows):
+            interleave(nc.vector.tensor_copy, words, rows, 0, VECTOR_SHARE)
+            interleave(nc.scalar.copy, words, rows, VECTOR_SHARE, W)
+
+        def quantise(name, words):
+            codes = sb.tile([P, W], U32, name=name + "_codes", align_bytes=64)
+            scales = sb.tile([P, W], U8, name=name + "_scales", align_bytes=64)
             nc.vector.quantize_mx(
                 out=codes[:].bitcast(FP8X4),
                 scales=scales[:],
-                in_=grouped[:].rearrange("p w j -> p (w j)"),
+                in_=words[:].rearrange("p w j -> p (w j)"),
             )
             return codes, scales
 
-        def product(banks, weights, moving, width):
-            for n0 in range(0, width, PASS):
-                cols = slice(n0, n0 + PASS)
-                for g in range(G):
-                    r = rows_of(g)
-                    nc.tensor.matmul_mx(
-                        out=banks[g][:, cols],
-                        lhsT=weights[0][r, :].bitcast(FP8X4),
-                        lhsT_scale=weights[1][r, :],
-                        rhs=moving[0][r, cols].bitcast(FP8X4),
-                        rhs_scale=moving[1][r, cols],
-                        start=True,
-                        stop=True,
-                    )
+        def product(banks, weights, moving):
+            for g in ALL_GROUPS:
+                r = rows_of(g)
+                nc.tensor.matmul_mx(
+                    out=banks[g][:, 0:W],
+                    lhsT=weights[0][r, :].bitcast(FP8X4),
+                    lhsT_scale=weights[1][r, :],
+                    rhs=moving[0][r, :].bitcast(FP8X4),
+                    rhs_scale=moving[1][r, :],
+                    start=True,
+                    stop=True,
+                )
 
-        bank_a = [ps.tile([P, 512], F32, name="bank_a%d" % g) for g in range(G)]
-        bank_b = [ps.tile([P, 512], F32, name="bank_b%d" % g) for g in range(G)]
+        bank_a = [ps.tile([P, BANK], F32, name="bank_a%d" % g) for g in ALL_GROUPS]
+        bank_b = [ps.tile([P, BANK], F32, name="bank_b%d" % g) for g in ALL_GROUPS]
 
         const_rows = sb.tile([P, 2 * M], F32, name="const_rows", align_bytes=64)
         nc.vector.memset(const_rows[:], 0.0)
+
         warm_in = sb.tile([P, 1], F32, name="warm_in")
         warm_out = sb.tile([P, 1], F32, name="warm_out")
-        nc.gpsimd.memset(warm_in[:], 1.0)
+        nc.vector.memset(warm_in[:], 1.0)
         nc.scalar.activation(out=warm_out[:], in_=warm_in[:], func=ACT.Abs_reciprocal_sqrt)
 
-        x_packed = x.rearrange("g (p j) n -> (g p) j n", j=PACK)
-        w1_raw = load_packed("w1", w1.rearrange("g (p j) m -> (g p) j m", j=PACK), M)
-        x_raw = [load_packed("x0", x_packed[:, :, 0 : CHUNKS[0]], CHUNKS[0])]
-        w2_raw = load_packed("w2", w2.rearrange("g (p j) m -> (g p) j m", j=PACK), M)
+        x_view = x.rearrange("g (p j) n -> (g p) j n", j=PACK)
+        w1_rows = load_rows("w1", w1.rearrange("g (p j) m -> (g p) j m", j=PACK), M)
+        x0_rows = load_rows("x0", x_view[:, :, 0:W], W)
+        w2_rows = load_rows("w2", w2.rearrange("g (p j) m -> (g p) j m", j=PACK), M)
+        x1_rows = load_rows("x1", x_view[:, :, W : 2 * W], W)
         for k, vec in enumerate((so, hs)):
             nc.sync.dma_start(
                 out=const_rows[0:P:ROWS, k * M : (k + 1) * M].rearrange("a (g i) -> a g i", g=G),
                 in_=vec.rearrange("g (a i) o -> a g (i o)", i=ROWS),
             )
-        for c in range(1, last + 1):
-            x_raw.append(load_packed("x%d" % c, x_packed[:, :, starts[c] : starts[c] + CHUNKS[c]], CHUNKS[c]))
-        wo_raw = load_packed("wo", wo2.rearrange("g (p j) o -> (g p) j o", j=PACK), O)
+        x23_rows = load_rows("x23", x_view[:, :, 2 * W : N], 2 * W)
+        wo_rows = load_rows("wo", wo2.rearrange("g (p j) o -> (g p) j o", j=PACK), O)
         res_sb = sb.tile([P, G, N], F32, name="res_sb")
         nc.sync.dma_start(out=res_sb[:], in_=res.rearrange("g o n -> o g n"))
+        x_rows = [x0_rows, x1_rows, x23_rows[:, :, 0:W], x23_rows[:, :, W : 2 * W]]
 
-        w1_grouped = interleave(nc.vector.tensor_copy, "w1", w1_raw, M)
-        x_grouped = interleave(nc.scalar.copy, "x0", x_raw[0], CHUNKS[0])
-        w1_q = quantise("w1", w1_grouped, M)
-        x_q = quantise("x0", x_grouped, CHUNKS[0])
-        w2_grouped = interleave(nc.vector.tensor_copy, "w2", w2_raw, M)
-        product(bank_a, w1_q, x_q, CHUNKS[0])
         consts = sb.tile([P, 2 * M], F32, name="consts", align_bytes=64)
-        w2_q = quantise("w2", w2_grouped, M)
-        product(bank_b, w2_q, x_q, CHUNKS[0])
-        nc.vector.transpose(out=consts[:], in_=const_rows[:])
+        x_words = [word_tile("x%d" % c) for c in range(CHUNKS)]
+        w1_words, w2_words, wo_words = word_tile("w1"), word_tile("w2"), word_tile("wo")
+        hh_words = [word_tile("hh%d" % c) for c in range(CHUNKS)]
+        hh_rows = [sb.tile([P, PACK, W], BF16, name="hh%d_rows" % c, align_bytes=64) for c in range(CHUNKS)]
+        y = sb.tile([P, G, N], F32, name="y")
+        out_view = out.rearrange("g o n -> o g n")
+        z1, prod, square, inv_norm = {}, {}, {}, {}
 
-        planes = []
-        wo_q = None
-        for c, width in enumerate(CHUNKS):
-            z1, prod, sq, inv = [], [], [], []
-            for g in range(G):
-                t = sb.tile([P, width], F32, name="z1_%d_%d" % (c, g))
-                nc.scalar.copy(out=t[:], in_=bank_a[g][:, 0:width])
-                z1.append(t)
-            for g in range(G):
-                t = sb.tile([P, width], F32, name="prod_%d_%d" % (c, g))
-                nc.vector.tensor_tensor(out=t[:], in0=bank_b[g][:, 0:width], in1=z1[g][:], op=ALU.mult)
-                prod.append(t)
-            if c < last:
-                ahead = interleave(nc.vector.tensor_copy, "x%d" % (c + 1), x_raw[c + 1], CHUNKS[c + 1])
-            else:
-                ahead = interleave(nc.vector.tensor_copy, "wo", wo_raw, O)
-            for g in range(G):
-                t = sb.tile([P, width], F32, name="sq_%d_%d" % (c, g))
-                if g < SQUARES_ON_SCALAR[c]:
-                    nc.scalar.activation(out=t[:], in_=prod[g][:], func=ACT.Square)
-                else:
-                    nc.vector.tensor_tensor(out=t[:], in0=prod[g][:], in1=prod[g][:], op=ALU.mult)
-                sq.append(t)
-            if c < last:
-                x_q = quantise("x%d" % (c + 1), ahead, CHUNKS[c + 1])
-                product(bank_a, w1_q, x_q, CHUNKS[c + 1])
-                product(bank_b, w2_q, x_q, CHUNKS[c + 1])
-            else:
-                wo_q = quantise("wo", ahead, O)
-            for g in range(G):
-                t = sb.tile([P, width], F32, name="inv_%d_%d" % (c, g))
+        def copy_z1(c):
+            for g in ALL_GROUPS:
+                z1[c, g] = sb.tile([P, W], F32, name="z1_%d_%d" % (c, g))
+                nc.scalar.copy(out=z1[c, g][:], in_=bank_a[g][:, 0:W])
+
+        def multiply(c, groups):
+            for g in groups:
+                prod[c, g] = sb.tile([P, W], F32, name="prod_%d_%d" % (c, g))
+                nc.vector.tensor_tensor(out=prod[c, g][:], in0=bank_b[g][:, 0:W], in1=z1[c, g][:], op=ALU.mult)
+
+        def square_on_scalar(c, groups):
+            for g in groups:
+                square[c, g] = sb.tile([P, W], F32, name="square_%d_%d" % (c, g))
+                nc.scalar.activation(out=square[c, g][:], in_=prod[c, g][:], func=ACT.Square)
+
+        def square_on_vector(c, groups):
+            for g in groups:
+                square[c, g] = sb.tile([P, W], F32, name="square_%d_%d" % (c, g))
+                nc.vector.tensor_tensor(out=square[c, g][:], in0=prod[c, g][:], in1=prod[c, g][:], op=ALU.mult)
+
+        def inverse_norm(c):
+            for g in ALL_GROUPS:
+                inv_norm[c, g] = sb.tile([P, W], F32, name="inv_norm_%d_%d" % (c, g))
                 nc.scalar.activation(
-                    out=t[:], in_=sq[g][:], func=ACT.Abs_reciprocal_sqrt,
+                    out=inv_norm[c, g][:],
+                    in_=square[c, g][:],
+                    func=ACT.Abs_reciprocal_sqrt,
                     bias=consts[:, ROWS * g : ROWS * g + 1],
                 )
-                inv.append(t)
-            plane = sb.tile([P, PACK, width], BF16, name="planes_%d" % c, align_bytes=64)
-            for g in range(G):
-                t = sb.tile([P, width], BF16, name="hh_%d_%d" % (c, g), align_bytes=64)
+
+        def hidden(c, groups):
+            for g in groups:
+                hh = sb.tile([P, W], BF16, name="hh_%d_%d" % (c, g), align_bytes=64)
                 nc.vector.scalar_tensor_tensor(
-                    out=t[:], in0=prod[g][:], scalar=consts[:, M + ROWS * g : M + ROWS * g + 1],
-                    in1=inv[g][:], op0=ALU.mult, op1=ALU.mult,
+                    out=hh[:],
+                    in0=prod[c, g][:],
+                    scalar=consts[:, M + ROWS * g : M + ROWS * g + 1],
+                    in1=inv_norm[c, g][:],
+                    op0=ALU.mult,
+                    op1=ALU.mult,
                 )
-                nc.sync.dma_start(out=plane[rows_of(g), :, :], in_=t[:])
-            planes.append(plane)
+                nc.sync.dma_start(out=hh_rows[c][rows_of(g), :, :], in_=hh[:])
 
-        out_view = out.rearrange("g o n -> o g n")
+        def second_banks(c):
+            return bank_a if c % 2 == 0 else bank_b
 
-        def second(c, grouped):
-            hh_q = quantise("hh%d" % c, grouped, CHUNKS[c])
-            product(bank_a if c % 2 == 0 else bank_b, wo_q, hh_q, CHUNKS[c])
+        def second_product(c):
+            product(second_banks(c), wo_q, quantise("hh%d" % c, hh_words[c]))
 
-        def finish(c):
-            width = CHUNKS[c]
-            banks = bank_a if c % 2 == 0 else bank_b
-            cols = slice(starts[c], starts[c] + width)
-            y = sb.tile([P, G, width], F32, name="y_%d" % c)
-            for g in range(G):
-                nc.vector.tensor_tensor(out=y[:, g, :], in0=banks[g][:, 0:width], in1=res_sb[:, g, cols], op=ALU.add)
-            nc.sync.dma_start(out=out_view[:, :, cols], in_=y[:])
+        def finish(c, groups):
+            cols = slice(c * W, (c + 1) * W)
+            for g in groups:
+                nc.vector.tensor_tensor(
+                    out=y[:, g, cols], in0=second_banks(c)[g][:, 0:W], in1=res_sb[:, g, cols], op=ALU.add
+                )
+            nc.sync.dma_start(
+                out=out_view[:, groups.start : groups.stop, cols], in_=y[:, groups.start : groups.stop, cols]
+            )
 
-        grouped = [interleave(nc.scalar.copy, "hh%d" % c, planes[c], CHUNKS[c]) for c in range(last + 1)]
-        second(0, grouped[0])
-        for c in range(1, last + 1):
-            second(c, grouped[c])
-            finish(c - 1)
-        finish(last)
+        interleave(nc.vector.tensor_copy, w1_words, w1_rows, 0, M)
+        w1_q = quantise("w1", w1_words)
+        interleave_shared(x_words[0], x_rows[0])
+        x_q = quantise("x0", x_words[0])
+        product(bank_a, w1_q, x_q)
+        interleave_shared(w2_words, w2_rows)
+        w2_q = quantise("w2", w2_words)
+        product(bank_b, w2_q, x_q)
+
+        copy_z1(0)
+        interleave(nc.vector.tensor_copy, x_words[1], x_rows[1], 0, W)
+        nc.vector.transpose(out=consts[:], in_=const_rows[:])
+        x_q = quantise("x1", x_words[1])
+        product(bank_a, w1_q, x_q)
+        multiply(0, ALL_GROUPS)
+        product(bank_b, w2_q, x_q)
+        square_on_scalar(0, ALL_GROUPS)
+
+        copy_z1(1)
+        inverse_norm(0)
+        interleave(nc.vector.tensor_copy, x_words[2], x_rows[2], 0, W)
+        multiply(1, FIRST_GROUPS)
+        x_q = quantise("x2", x_words[2])
+        product(bank_a, w1_q, x_q)
+        multiply(1, LAST_GROUPS)
+        product(bank_b, w2_q, x_q)
+        square_on_scalar(1, ALL_GROUPS)
+        interleave(nc.vector.tensor_copy, x_words[3], x_rows[3], 0, W)
+        hidden(0, FIRST_GROUPS)
+        x_q = quantise("x3", x_words[3])
+        hidden(0, LAST_GROUPS)
+
+        copy_z1(2)
+        product(bank_a, w1_q, x_q)
+        multiply(2, ALL_GROUPS)
+        product(bank_b, w2_q, x_q)
+        inverse_norm(1)
+        copy_z1(3)
+        square_on_vector(2, FIRST_GROUPS)
+        square_on_scalar(2, LAST_GROUPS)
+        hidden(1, ALL_GROUPS)
+
+        multiply(3, ALL_GROUPS)
+        inverse_norm(2)
+        square_on_scalar(3, ALL_GROUPS)
+        hidden(2, ALL_GROUPS)
+        interleave(nc.vector.tensor_copy, wo_words, wo_rows, 0, O)
+        inverse_norm(3)
+        hidden(3, ALL_GROUPS)
+
+        for c in range(CHUNKS - 1):
+            interleave(nc.scalar.copy, hh_words[c], hh_rows[c], 0, W)
+        interleave(nc.scalar.copy, hh_words[3], hh_rows[3], VECTOR_SHARE, W)
+        wo_q = quantise("wo", wo_words)
+        second_product(0)
+        second_product(1)
+        finish(0, FIRST_GROUPS)
+        finish(0, LAST_GROUPS)
+        second_product(2)
+        finish(1, FIRST_GROUPS)
+        interleave(nc.vector.tensor_copy, hh_words[3], hh_rows[3], 0, VECTOR_SHARE)
+        finish(1, LAST_GROUPS)
+        second_product(3)
+        for c in range(2, CHUNKS):
+            finish(c, FIRST_GROUPS)
+            finish(c, LAST_GROUPS)

from contextlib import ExitStack

import concourse.mybir as mybir

G, D, M, O, N = 4, 128, 128, 128, 512
FLOPS = 2 * G * N * (2 * D * M + M * O)

F32 = mybir.dt.float32
BF16 = mybir.dt.bfloat16
U32 = mybir.dt.uint32
U8 = mybir.dt.uint8
FP8X4 = mybir.dt.float8_e4m3fn_x4
ACT = mybir.ActivationFunctionType
ALU = mybir.AluOpType

P = 128
PACK = 4
ROWS = 32
W = 128
CHUNKS = N // W
BANK = 512
RUN = 4
VECTOR_SHARE = 80
HALF = G // 2
ALL_GROUPS = range(G)
FIRST_GROUPS = range(HALF)
LAST_GROUPS = range(HALF, G)


def tile_rows_fagree_kernel(tc, x, w1, w2, so, hs, wo2, res, out):
    nc = tc.nc

    with ExitStack() as ctx:
        sb = ctx.enter_context(tc.tile_pool(name="sb", bufs=1))
        ps = ctx.enter_context(tc.psum_pool(name="ps", bufs=1))
        ctx.enter_context(tc.manual_schedule())

        def rows_of(g):
            return slice(ROWS * g, ROWS * (g + 1))

        def load_rows(name, src, width):
            rows = sb.tile([P, PACK, width], F32, name=name + "_rows", align_bytes=64)
            nc.sync.dma_start(out=rows[:], in_=src)
            return rows

        def word_tile(name):
            return sb.tile([P, W, PACK], BF16, name=name + "_words", align_bytes=64)

        def interleave(copy, words, rows, lo, hi):
            copy(
                out=words[:, lo:hi, :].rearrange("p (c i) j -> p c j i", i=RUN),
                in_=rows[:, :, lo:hi].rearrange("p j (c i) -> p c j i", i=RUN),
            )

        def interleave_shared(words, rows):
            interleave(nc.vector.tensor_copy, words, rows, 0, VECTOR_SHARE)
            interleave(nc.scalar.copy, words, rows, VECTOR_SHARE, W)

        def quantise(name, words):
            codes = sb.tile([P, W], U32, name=name + "_codes", align_bytes=64)
            scales = sb.tile([P, W], U8, name=name + "_scales", align_bytes=64)
            nc.vector.quantize_mx(
                out=codes[:].bitcast(FP8X4),
                scales=scales[:],
                in_=words[:].rearrange("p w j -> p (w j)"),
            )
            return codes, scales

        def product(banks, weights, moving):
            for g in ALL_GROUPS:
                r = rows_of(g)
                nc.tensor.matmul_mx(
                    out=banks[g][:, 0:W],
                    lhsT=weights[0][r, :].bitcast(FP8X4),
                    lhsT_scale=weights[1][r, :],
                    rhs=moving[0][r, :].bitcast(FP8X4),
                    rhs_scale=moving[1][r, :],
                    start=True,
                    stop=True,
                )

        bank_a = [ps.tile([P, BANK], F32, name="bank_a%d" % g) for g in ALL_GROUPS]
        bank_b = [ps.tile([P, BANK], F32, name="bank_b%d" % g) for g in ALL_GROUPS]

        const_rows = sb.tile([P, 2 * M], F32, name="const_rows", align_bytes=64)
        nc.vector.memset(const_rows[:], 0.0)

        warm_in = sb.tile([P, 1], F32, name="warm_in")
        warm_out = sb.tile([P, 1], F32, name="warm_out")
        nc.vector.memset(warm_in[:], 1.0)
        nc.scalar.activation(out=warm_out[:], in_=warm_in[:], func=ACT.Abs_reciprocal_sqrt)

        x_view = x.rearrange("g (p j) n -> (g p) j n", j=PACK)
        w1_rows = load_rows("w1", w1.rearrange("g (p j) m -> (g p) j m", j=PACK), M)
        x0_rows = load_rows("x0", x_view[:, :, 0:W], W)
        w2_rows = load_rows("w2", w2.rearrange("g (p j) m -> (g p) j m", j=PACK), M)
        x1_rows = load_rows("x1", x_view[:, :, W : 2 * W], W)
        for k, vec in enumerate((so, hs)):
            nc.sync.dma_start(
                out=const_rows[0:P:ROWS, k * M : (k + 1) * M].rearrange("a (g i) -> a g i", g=G),
                in_=vec.rearrange("g (a i) o -> a g (i o)", i=ROWS),
            )
        x23_rows = load_rows("x23", x_view[:, :, 2 * W : N], 2 * W)
        wo_rows = load_rows("wo", wo2.rearrange("g (p j) o -> (g p) j o", j=PACK), O)
        res_sb = sb.tile([P, G, N], F32, name="res_sb")
        nc.sync.dma_start(out=res_sb[:], in_=res.rearrange("g o n -> o g n"))
        x_rows = [x0_rows, x1_rows, x23_rows[:, :, 0:W], x23_rows[:, :, W : 2 * W]]

        consts = sb.tile([P, 2 * M], F32, name="consts", align_bytes=64)
        x_words = [word_tile("x%d" % c) for c in range(CHUNKS)]
        w1_words, w2_words, wo_words = word_tile("w1"), word_tile("w2"), word_tile("wo")
        hh_words = [word_tile("hh%d" % c) for c in range(CHUNKS)]
        hh_rows = [sb.tile([P, PACK, W], BF16, name="hh%d_rows" % c, align_bytes=64) for c in range(CHUNKS)]
        y = sb.tile([P, G, N], F32, name="y")
        out_view = out.rearrange("g o n -> o g n")
        z1, prod, square, inv_norm = {}, {}, {}, {}

        def copy_z1(c):
            for g in ALL_GROUPS:
                z1[c, g] = sb.tile([P, W], F32, name="z1_%d_%d" % (c, g))
                nc.scalar.copy(out=z1[c, g][:], in_=bank_a[g][:, 0:W])

        def multiply(c, groups):
            for g in groups:
                prod[c, g] = sb.tile([P, W], F32, name="prod_%d_%d" % (c, g))
                nc.vector.tensor_tensor(out=prod[c, g][:], in0=bank_b[g][:, 0:W], in1=z1[c, g][:], op=ALU.mult)

        def square_on_scalar(c, groups):
            for g in groups:
                square[c, g] = sb.tile([P, W], F32, name="square_%d_%d" % (c, g))
                nc.scalar.activation(out=square[c, g][:], in_=prod[c, g][:], func=ACT.Square)

        def square_on_vector(c, groups):
            for g in groups:
                square[c, g] = sb.tile([P, W], F32, name="square_%d_%d" % (c, g))
                nc.vector.tensor_tensor(out=square[c, g][:], in0=prod[c, g][:], in1=prod[c, g][:], op=ALU.mult)

        def inverse_norm(c):
            for g in ALL_GROUPS:
                inv_norm[c, g] = sb.tile([P, W], F32, name="inv_norm_%d_%d" % (c, g))
                nc.scalar.activation(
                    out=inv_norm[c, g][:],
                    in_=square[c, g][:],
                    func=ACT.Abs_reciprocal_sqrt,
                    bias=consts[:, ROWS * g : ROWS * g + 1],
                )

        def hidden(c, groups):
            for g in groups:
                hh = sb.tile([P, W], BF16, name="hh_%d_%d" % (c, g), align_bytes=64)
                nc.vector.scalar_tensor_tensor(
                    out=hh[:],
                    in0=prod[c, g][:],
                    scalar=consts[:, M + ROWS * g : M + ROWS * g + 1],
                    in1=inv_norm[c, g][:],
                    op0=ALU.mult,
                    op1=ALU.mult,
                )
                nc.sync.dma_start(out=hh_rows[c][rows_of(g), :, :], in_=hh[:])

        def second_banks(c):
            return bank_a if c % 2 == 0 else bank_b

        def second_product(c):
            product(second_banks(c), wo_q, quantise("hh%d" % c, hh_words[c]))

        def finish(c, groups):
            cols = slice(c * W, (c + 1) * W)
            for g in groups:
                nc.vector.tensor_tensor(
                    out=y[:, g, cols], in0=second_banks(c)[g][:, 0:W], in1=res_sb[:, g, cols], op=ALU.add
                )
            nc.sync.dma_start(
                out=out_view[:, groups.start : groups.stop, cols], in_=y[:, groups.start : groups.stop, cols]
            )

        interleave(nc.vector.tensor_copy, w1_words, w1_rows, 0, M)
        w1_q = quantise("w1", w1_words)
        interleave_shared(x_words[0], x_rows[0])
        x_q = quantise("x0", x_words[0])
        product(bank_a, w1_q, x_q)
        interleave_shared(w2_words, w2_rows)
        w2_q = quantise("w2", w2_words)
        product(bank_b, w2_q, x_q)

        copy_z1(0)
        interleave(nc.vector.tensor_copy, x_words[1], x_rows[1], 0, W)
        nc.vector.transpose(out=consts[:], in_=const_rows[:])
        x_q = quantise("x1", x_words[1])
        product(bank_a, w1_q, x_q)
        multiply(0, ALL_GROUPS)
        product(bank_b, w2_q, x_q)
        square_on_scalar(0, ALL_GROUPS)

        copy_z1(1)
        inverse_norm(0)
        interleave(nc.vector.tensor_copy, x_words[2], x_rows[2], 0, W)
        multiply(1, FIRST_GROUPS)
        x_q = quantise("x2", x_words[2])
        product(bank_a, w1_q, x_q)
        multiply(1, LAST_GROUPS)
        product(bank_b, w2_q, x_q)
        square_on_scalar(1, ALL_GROUPS)
        interleave(nc.vector.tensor_copy, x_words[3], x_rows[3], 0, W)
        hidden(0, FIRST_GROUPS)
        x_q = quantise("x3", x_words[3])
        hidden(0, LAST_GROUPS)

        copy_z1(2)
        product(bank_a, w1_q, x_q)
        multiply(2, ALL_GROUPS)
        product(bank_b, w2_q, x_q)
        inverse_norm(1)
        copy_z1(3)
        square_on_vector(2, FIRST_GROUPS)
        square_on_scalar(2, LAST_GROUPS)
        hidden(1, ALL_GROUPS)

        multiply(3, ALL_GROUPS)
        inverse_norm(2)
        square_on_scalar(3, ALL_GROUPS)
        hidden(2, ALL_GROUPS)
        interleave(nc.vector.tensor_copy, wo_words, wo_rows, 0, O)
        inverse_norm(3)
        hidden(3, ALL_GROUPS)

        for c in range(CHUNKS - 1):
            interleave(nc.scalar.copy, hh_words[c], hh_rows[c], 0, W)
        interleave(nc.scalar.copy, hh_words[3], hh_rows[3], VECTOR_SHARE, W)
        wo_q = quantise("wo", wo_words)
        second_product(0)
        second_product(1)
        finish(0, FIRST_GROUPS)
        finish(0, LAST_GROUPS)
        second_product(2)
        finish(1, FIRST_GROUPS)
        interleave(nc.vector.tensor_copy, hh_words[3], hh_rows[3], 0, VECTOR_SHARE)
        finish(1, LAST_GROUPS)
        second_product(3)
        for c in range(2, CHUNKS):
            finish(c, FIRST_GROUPS)
            finish(c, LAST_GROUPS)
